import numpy as np
import ml_dtypes


def mxq(x, axis, fmt="e4m3"):
    dtype, down = {"e4m3": (ml_dtypes.float8_e4m3fn, 7), "e5m2": (ml_dtypes.float8_e5m2, 14)}[fmt]
    v = np.moveaxis(np.asarray(x, np.float32).astype(ml_dtypes.bfloat16).astype(np.float64), axis, -1)
    blocks = v.reshape(v.shape[:-1] + (-1, 32))
    amax = np.abs(blocks).max(-1, keepdims=True)
    byte = np.maximum(np.where(amax > 0, np.frexp(amax)[1] - 1 + 127, 0) - down, 1)
    scale = np.exp2(byte - 127.0)
    codes = (blocks / scale).astype(np.float32).astype(dtype).astype(np.float64)
    return np.moveaxis((codes * scale).reshape(v.shape), -1, axis)


WIDE = False


def mx_kscale(k):
    if not WIDE:
        return np.ones(k)
    levels = np.array([10, -10, 5, -5, 0])
    if k % 512:
        return np.exp2(np.random.permutation(np.resize(levels, k // 32))).repeat(32)
    a = np.empty((k // 512, 16))
    for p in range(k // 512):
        a[p, :8] = np.random.permutation(np.resize(levels, 8))
        for g in range(8):
            far = levels[np.abs(levels - a[p, g]) >= 10]
            a[p, g + 8] = far[np.random.randint(len(far))]
    return np.exp2(a.ravel()).repeat(32)


BF16 = ml_dtypes.bfloat16


def bf(x):
    return np.asarray(x, np.float32).astype(BF16)


def f64(x):
    return np.asarray(x).astype(np.float64)


E2M1 = np.array([0.0, 0.5, 1.0, 1.5, 2.0, 3.0, 4.0, 6.0, -0.0, -0.5, -1.0, -1.5, -2.0, -3.0, -4.0, -6.0])


def pack_weight(w, fmt):
    k, n = w.shape
    w = f64(bf(w)).reshape(k // 32, 32, n)
    amax = np.abs(w).max(1)
    if fmt == "e4m3":
        byte = np.frexp(amax)[1] - 1 + 127 - 7
    else:
        mant, ex = np.frexp(amax / 6.0)
        byte = np.where(mant > 0.5, ex, ex - 1) + 127
    byte = np.clip(np.where(amax > 0, byte, 1), 1, 254)
    scaled = (w * np.exp2(127.0 - byte)[:, None, :]).reshape(k, n).astype(np.float32)
    by_word = np.ascontiguousarray(scaled.reshape(k // 512, 128, 4, n).transpose(0, 1, 3, 2))
    if fmt == "e4m3":
        words = by_word.astype(ml_dtypes.float8_e4m3fn).view(np.uint8)
    else:
        c = by_word.astype(ml_dtypes.float4_e2m1fn).view(np.uint8) & 0xF
        words = c[..., 0::2] | (c[..., 1::2] << 4)
    return np.ascontiguousarray(words), np.ascontiguousarray(byte.astype(np.uint8).reshape(k // 512, 16, n))


def unpack_weight(words, scales, fmt):
    g, p, n, _ = words.shape
    if fmt == "e4m3":
        vals = np.ascontiguousarray(words).view(ml_dtypes.float8_e4m3fn).astype(np.float64)
    else:
        nib = np.empty((g, p, n, 4), np.uint8)
        nib[..., 0::2] = words & 0xF
        nib[..., 1::2] = words >> 4
        vals = E2M1[nib]
    vals = vals * np.repeat(np.exp2(scales.astype(np.float64) - 127.0), 8, axis=1)[..., None]
    return vals.transpose(0, 1, 3, 2).reshape(g * 512, n)
def pack4(w):
    words, scales = pack_weight(w, "e2m1")
    return words.reshape(words.shape[0], 128, -1), scales


def unpack4(words, scales):
    return unpack_weight(words.reshape(words.shape[0], 128, -1, 2), scales, "e2m1")


E4M3FN = np.array([(-1.0 if i & 128 else 1.0) * ((1.0 + (i & 7) / 8.0) * 2.0 ** (((i >> 3) & 15) - 7) if i & 120 else (i & 7) * 2.0 ** -9) for i in range(256)])


def e4m3fn_bytes(y):
    return np.clip(np.asarray(y, np.float64), -448.0, 448.0).astype(np.float32).astype(ml_dtypes.float8_e4m3fn).view(np.uint8)


def e4m3fn_values(b):
    return E4M3FN[b]


L, K, F, J, BLK = 1024, 2560, 1024, 2048, 128


def setup_inputs():
    s, t = mx_kscale(K), mx_kscale(F)
    x = np.random.standard_normal((L, K)) * s
    x_scale = (np.abs(x).reshape(L, K // BLK, BLK).max(axis=2) / 448).astype(np.float32)
    x_bytes = e4m3fn_bytes(x / np.repeat(f64(x_scale), BLK, axis=1))
    u_words, u_scales = pack4(np.random.standard_normal((F, J)) / np.sqrt(F) / t[:, None])
    return {"x_bytes": x_bytes,
            "x_scale": x_scale,
            "w": bf(np.random.standard_normal((K, F)) / np.sqrt(K) / s[:, None] * t),
            "b": bf(0.3 * np.random.standard_normal(F) * t),
            "v": bf(np.random.uniform(0.5, 1.0, L)),
            "u_words": u_words,
            "u_scales": u_scales,
            "c": bf(0.3 * np.random.standard_normal(J))}


def reference(x_bytes, x_scale, w, b, v, u_words, u_scales, c):
    x = e4m3fn_values(x_bytes) * np.repeat(f64(x_scale), BLK, axis=1)
    y = mxq(x, 1, "e4m3") @ mxq(f64(w), 0, "e4m3")
    h = (y + f64(b)) * f64(v)[:, None]
    z = unpack4(u_words, u_scales).T @ mxq(h, 1, "e4m3").T
    return z + f64(c)[:, None]

@@ -1,0 +1,438 @@
+from contextlib import ExitStack
+
+import concourse.mybir as mybir
+from concourse.masks import make_identity
+
+L, K, F, J = 1024, 2560, 1024, 2048
+FLOPS = 2 * L * K * F + 2 * J * F * L
+
+F32 = mybir.dt.float32
+BF16 = mybir.dt.bfloat16
+U8 = mybir.dt.uint8
+U32 = mybir.dt.uint32
+I32 = mybir.dt.int32
+E4M3 = mybir.dt.float8_e4m3fn
+E4M3X4 = mybir.dt.float8_e4m3fn_x4
+E2M1X4 = mybir.dt.float4_e2m1fn_x4
+MULT = mybir.AluOpType.mult
+ADD = mybir.AluOpType.add
+COPY = mybir.ActivationFunctionType.Copy
+IDENT = mybir.ActivationFunctionType.Identity
+
+P = 128
+PASSES = K // 512
+HALF = 512
+GROUPS = F // 512
+WG = {"V": 2, "S": 3}
+
+
+def tile_biaffine_contact_transposed_d4_kernel(tc, x_bytes, x_scale, w, b, v, u_words, u_scales, c, out):
+    nc = tc.nc
+    with ExitStack() as ctx:
+        keep = ctx.enter_context(tc.tile_pool(name="keep", bufs=1))
+        work = ctx.enter_context(tc.tile_pool(name="work", bufs=2))
+        psum = ctx.enter_context(tc.psum_pool(name="psum", bufs=1))
+
+        def bank(i):
+            return psum.tile([P, 512], F32, name="bank%d" % i)
+
+        x_sc = keep.tile([P, 8, 20], F32, name="x_sc")
+        ident = keep.tile([P, P], F32, name="ident")
+        ones = keep.tile([P, P], BF16, name="ones")
+        v_row = keep.tile([P, L], BF16, name="v_row")
+        v_all = keep.tile([P, L], F32, name="v_all")
+        b_raw = keep.tile([P, GROUPS, 4], BF16, name="b_raw")
+        b_col = keep.tile([P, GROUPS, 4], F32, name="b_col")
+        c_raw = keep.tile([16, P], BF16, name="c_raw")
+        c_row = keep.tile([P, P], F32, name="c_row")
+        c_col = keep.tile([P, 16], F32, name="c_col")
+        x_codes = keep.tile([P, PASSES, L], U32, name="x_codes", align_bytes=64)
+        x_planes = keep.tile([P, PASSES, L], U8, name="x_planes", align_bytes=64)
+        w_codes = keep.tile([P, PASSES, F], U32, name="w_codes", align_bytes=64)
+        w_planes = keep.tile([P, PASSES, F], U8, name="w_planes", align_bytes=64)
+        h_codes = keep.tile([P, GROUPS, L], U32, name="h_codes", align_bytes=64)
+        h_planes = keep.tile([P, GROUPS, L], U8, name="h_planes", align_bytes=64)
+        u_w = keep.tile([P, GROUPS, 2 * J], U8, name="u_w", align_bytes=64)
+        u_s = keep.tile([P, GROUPS, J], U8, name="u_s", align_bytes=64)
+
+        with tc.manual_schedule():
+            make_identity(nc, ident[:])
+            nc.gpsimd.memset(v_row[:], 0.0)
+            nc.gpsimd.memset(c_row[:], 0.0)
+            nc.gpsimd.memset(ones[:], 1.0)
+            nc.gpsimd.memset(u_s[:].rearrange("p g n -> p (g n)").bitcast(I32), 0)
+
+            nc.scalar.dma_start(out=x_sc[:], in_=x_scale.rearrange("(r p) d -> p r d", p=P))
+            xb = []
+            for r in range(8):
+                xb.append(work.tile([P, K], U8, name="xb", bufs=8))
+            wr = []
+
+            def load_x(r):
+                nc.sync.dma_start(out=xb[r][:], in_=x_bytes[P * r : P * r + P, :])
+
+            def load_w(g):
+                t = work.tile([P, 4, F], BF16, name="wr%d" % g, bufs=1)
+                nc.sync.dma_start(out=t[:], in_=w[512 * g : 512 * g + 512, :].rearrange("(p j) f -> p j f", j=4))
+                wr.append(t)
+
+            for r in range(4):
+                load_x(r)
+            nc.gpsimd.dma_start(out=v_row[0:1, :], in_=v.rearrange("(o i) -> o i", o=1))
+            nc.gpsimd.dma_start(out=c_raw[:], in_=c.rearrange("(j p) -> j p", p=P))
+            nc.gpsimd.dma_start(out=b_raw[:], in_=b.rearrange("(g p t) -> p g t", p=P, t=4))
+            nc.gpsimd.tensor_copy(out=c_row[0:16, :], in_=c_raw[:])
+            nc.gpsimd.tensor_copy(out=b_col[:], in_=b_raw[:])
+            for g in range(PASSES):
+                load_w(g)
+            for r in range(4, 8):
+                load_x(r)
+            for g in range(GROUPS):
+                nc.sync.dma_start(out=u_w[:, g, :].bitcast(I32), in_=u_words[g].bitcast(I32))
+            for q in range(4):
+                nc.sync.dma_start(
+                    out=u_s[32 * q : 32 * q + 4, :, :].bitcast(I32),
+                    in_=u_scales[:, 4 * q : 4 * q + 4, :].rearrange("g q n -> q g n").bitcast(I32),
+                )
+
+            xw, xg, wg, hs, hg, o_tile = {}, {}, {}, {}, {}, {}
+            bank_of = {}
+            wg_count = {"V": 0, "S": 0}
+
+            def widen(eng, pair, g):
+                for r in (2 * pair, 2 * pair + 1):
+                    if r not in xw:
+                        xw[r] = work.tile([P, PASSES, 2, P, 2], BF16, name="xw%d" % (r % 4), bufs=1, align_bytes=64)
+                    for q in range(4):
+                        d = 4 * g + q
+                        byte = xb[r][:, 128 * d : 128 * d + 128].bitcast(E4M3)
+                        if eng == "S":
+                            nc.scalar.activation(
+                                out=xw[r][:, g, :, :, :].rearrange("p u m e -> p (u m e)")[:, 128 * q : 128 * q + 128],
+                                in_=byte,
+                                func=COPY,
+                                scale=x_sc[:, r, d : d + 1],
+                            )
+                        else:
+                            nc.vector.tensor_scalar(
+                                out=xw[r][:, g, :, 32 * q : 32 * q + 32, :].rearrange("p u m e -> p m u e"),
+                                in0=byte.rearrange("p (m u e) -> p m u e", u=2, e=2),
+                                scalar1=x_sc[:, r, d : d + 1],
+                                scalar2=None,
+                                op0=MULT,
+                            )
+
+            def turn(eng, pair, g):
+                bank_of["T", pair, g] = bank(place["T", pair, g])
+                tv = bank_of["T", pair, g][:].rearrange("p (u r) -> p u r", u=2)
+                for k, r in enumerate((2 * pair, 2 * pair + 1)):
+                    for u in range(2):
+                        if ("A", pair, g) in on_s:
+                            words = xw[r][:, g, :, :, :].rearrange("p u m e -> p (u m e)").bitcast(F32)[:, u::2]
+                        else:
+                            words = xw[r][:, g, u, :, :].rearrange("p m e -> p (m e)").bitcast(F32)
+                        nc.tensor.transpose(tv[:, u, P * k : P * k + P], words, ident[:])
+
+            def x_out(eng, pair, g):
+                h, k = pair // 2, pair % 2
+                if (h, g) not in xg:
+                    xg[h, g] = work.tile([P, HALF, 4], BF16, name="xg%d" % g, bufs=1, align_bytes=64)
+                dst = xg[h, g][:, 256 * k : 256 * k + 256, :].rearrange("p r j -> p (r j)").bitcast(F32).rearrange("p (r u) -> p r u", u=2)
+                src = bank_of["T", pair, g][:].rearrange("p (u r) -> p r u", u=2)
+                if eng == "S":
+                    nc.scalar.copy(out=dst, in_=src)
+                else:
+                    nc.vector.tensor_copy(out=dst, in_=src)
+
+            def x_quant(eng, h, g):
+                nc.vector.quantize_mx(
+                    out=x_codes[:, g, HALF * h : HALF * h + HALF].bitcast(E4M3X4),
+                    scales=x_planes[:, g, HALF * h : HALF * h + HALF],
+                    in_=xg[h, g][:].rearrange("p r j -> p (r j)"),
+                )
+
+            def w_mix(eng, g, G):
+                t = work.tile([P, 4, P, 4], BF16, name="wg%s%d" % (eng, wg_count[eng] % WG[eng]), bufs=1, align_bytes=64)
+                wg_count[eng] += 1
+                wg[g, G] = t
+                src = wr[g][:, :, 512 * G : 512 * G + 512].rearrange("p j (m t) -> p t m j", t=4)
+                if eng == "S":
+                    nc.scalar.copy(out=t[:], in_=src)
+                else:
+                    nc.vector.tensor_copy(out=t[:], in_=src)
+
+            def w_quant(eng, g, G):
+                nc.vector.quantize_mx(
+                    out=w_codes[:, g, 512 * G : 512 * G + 512].bitcast(E4M3X4),
+                    scales=w_planes[:, g, 512 * G : 512 * G + 512],
+                    in_=wg[g, G][:].rearrange("p t m j -> p (t m j)"),
+                )
+
+            def spread(eng):
+                bank_of["v0"], bank_of["v1"], bank_of["c"] = bank(6), bank(7), bank(5)
+                for k in range(2):
+                    nc.tensor.matmul(bank_of["v%d" % k][:], lhsT=ones[:], rhs=v_row[:, 512 * k : 512 * k + 512], start=True, stop=True)
+                nc.tensor.transpose(bank_of["c"][:, 0:P], c_row[:], ident[:])
+
+            def spread_out(eng):
+                for k in range(2):
+                    nc.scalar.copy(out=v_all[:, 512 * k : 512 * k + 512], in_=bank_of["v%d" % k][:])
+                nc.scalar.copy(out=c_col[:], in_=bank_of["c"][:, 0:16])
+
+            def mul1(eng, h, G, t, g):
+                if g == passes[h, G][0]:
+                    bank_of[h, G, t] = bank(place["Y", h, G, t])
+                col = 512 * G + P * t
+                nc.tensor.matmul_mx(
+                    out=bank_of[h, G, t][:],
+                    lhsT=w_codes[:, g, col : col + P].bitcast(E4M3X4),
+                    lhsT_scale=w_planes[:, g, col : col + P],
+                    rhs=x_codes[:, g, HALF * h : HALF * h + HALF].bitcast(E4M3X4),
+                    rhs_scale=x_planes[:, g, HALF * h : HALF * h + HALF],
+                    start=(g == passes[h, G][0]),
+                    stop=(g == passes[h, G][-1]),
+                )
+
+            def h_bias(eng, h, G, t):
+                if eng == "S":
+                    if t == 0:
+                        hs[h, G] = work.tile([P, 4, HALF], F32, name="hs", bufs=2)
+                    nc.scalar.activation(out=hs[h, G][:, t, :], in_=bank_of[h, G, t][:], func=IDENT, bias=b_col[:, G, t : t + 1], scale=1.0)
+                else:
+                    if t == 0:
+                        hs[h, G] = work.tile([P, 4, HALF], BF16, name="hb", bufs=2)
+                    nc.vector.scalar_tensor_tensor(
+                        out=hs[h, G][:, t, :],
+                        in0=bank_of[h, G, t][:],
+                        scalar=b_col[:, G, t : t + 1],
+                        in1=v_all[:, HALF * h : HALF * h + HALF],
+                        op0=ADD,
+                        op1=MULT,
+                    )
+
+            def h_mix(eng, h, G, k):
+                s = HALF // 2
+                if (h, G) not in hg:
+                    hg[h, G] = work.tile([P, HALF, 4], BF16, name="hg", bufs=2, align_bytes=64)
+                dst = hg[h, G][:, s * k : s * k + s, :]
+                src = hs[h, G][:, :, s * k : s * k + s].rearrange("p t i -> p i t")
+                if ("E", h, G, 0) not in on_s:
+                    if eng == "S":
+                        nc.scalar.copy(out=dst, in_=src)
+                    else:
+                        nc.vector.tensor_copy(out=dst, in_=src)
+                else:
+                    nc.vector.tensor_tensor(
+                        out=dst,
+                        in0=src,
+                        in1=v_all[:, HALF * h + s * k : HALF * h + s * k + s].unsqueeze(2).to_broadcast([P, s, 4]),
+                        op=MULT,
+                    )
+
+            def h_quant(eng, h, G):
+                nc.vector.quantize_mx(
+                    out=h_codes[:, G, HALF * h : HALF * h + HALF].bitcast(E4M3X4),
+                    scales=h_planes[:, G, HALF * h : HALF * h + HALF],
+                    in_=hg[h, G][:].rearrange("p i t -> p (i t)"),
+                )
+
+            def mul2(eng, h, jt, G):
+                if G == 0:
+                    bank_of["O", h, jt] = bank(place["O", h, jt])
+                nc.tensor.matmul_mx(
+                    out=bank_of["O", h, jt][:],
+                    lhsT=u_w[:, G, 256 * jt : 256 * jt + 256].bitcast(E2M1X4),
+                    lhsT_scale=u_s[:, G, P * jt : P * jt + P],
+                    rhs=h_codes[:, G, HALF * h : HALF * h + HALF].bitcast(E4M3X4),
+                    rhs_scale=h_planes[:, G, HALF * h : HALF * h + HALF],
+                    start=(G == 0),
+                    stop=(G == GROUPS - 1),
+                )
+
+            def finish(eng, h, jt):
+                i = zq.index((h, jt))
+                if i // 4 not in o_tile:
+                    o_tile[i // 4] = work.tile([P, 4, HALF], F32, name="wr%d" % (i // 4 % 5), bufs=1)
+                t = o_tile[i // 4][:, i % 4, :]
+                if eng == "S":
+                    nc.scalar.activation(out=t, in_=bank_of["O", h, jt][:], func=IDENT, bias=c_col[:, jt : jt + 1], scale=1.0)
+                else:
+                    nc.vector.tensor_scalar(out=t, in0=bank_of["O", h, jt][:], scalar1=c_col[:, jt : jt + 1], scalar2=None, op0=ADD)
+
+            def store(eng, h, jt):
+                nc.sync.dma_start(out=out[P * jt : P * jt + P, HALF * h : HALF * h + HALF], in_=o_tile[zq.index((h, jt)) // 4][:, zq.index((h, jt)) % 4, :])
+
+            vec, sca, pe, place = [], [], [], {}
+            on_s = {("A", pair, 4) for pair in range(4)}
+            passes = {(h, G): (0, 1, 2, 3, 4) for h in range(2) for G in range(2)}
+            passes[0, 1] = (0, 3, 1, 4, 2)
+            passes[1, 0] = passes[1, 1] = (4, 0, 1, 2, 3)
+
+            def a(q, *ss):
+                q.extend(ss)
+
+            a(sca, ("A", 0, 4))
+            for g in range(4):
+                a(vec, ("A", 0, g))
+            for g in range(4):
+                a(vec, ("A", 1, g))
+            for g in range(5):
+                a(pe, ("T", 0, g))
+            for g in range(5):
+                a(pe, ("T", 1, g))
+            for i in range(10):
+                place["T", i // 5, i % 5] = i % 5
+            a(sca, ("B", 0, 0), ("B", 0, 1), ("A", 1, 4))
+            a(sca, ("B", 0, 2), ("B", 0, 3), ("B", 0, 4))
+            for g in range(5):
+                a(sca, ("B", 1, g))
+            a(pe, ("K",))
+            a(vec, ("C", 0, 0), ("X", 0, 0), ("X", 0, 1), ("W", 0, 0), ("X", 0, 2), ("C", 2, 0), ("W", 1, 0), ("X", 0, 3), ("X", 0, 4), ("W", 2, 0))
+            a(sca, ("C", 1, 0), ("C", 0, 1), ("C", 3, 0), ("k",))
+            a(vec, ("W", 0, 1), ("C", 4, 0), ("W", 3, 0), ("W", 4, 0))
+            a(sca, ("C", 1, 1), ("C", 2, 1))
+            a(vec, ("C", 3, 1), ("C", 4, 1), ("W", 3, 1), ("W", 1, 1), ("W", 4, 1))
+            for t in range(4):
+                a(vec, ("E", 0, 0, t))
+            a(vec, ("W", 2, 1))
+            for G in range(2):
+                for g in passes[0, G]:
+                    for t in range(4):
+                        a(pe, ("Y", 0, G, t, g))
+            for G in range(2):
+                for t in range(4):
+                    place["Y", 0, G, t] = 4 * G + t
+                    place["Y", 1, G, t] = 4 * (1 - G) + t
+            a(sca, ("A", 2, 4), ("A", 3, 4))
+            a(sca, ("M", 0, 0, 0), ("M", 0, 0, 1))
+            n = 0
+            order = (4, 0, 1, 2, 3)
+            for i, g in enumerate(order):
+                for pair in (2, 3):
+                    if g != 4:
+                        a(vec, ("A", pair, g))
+                    a(pe, ("T", pair, g))
+                    place["T", pair, g] = n % 4
+                    a(sca, ("B", pair, g))
+                    n += 1
+                if i == 2:
+                    for t in range(4):
+                        a(vec, ("E", 0, 1, t))
+                if i >= 2:
+                    a(vec, ("X", 1, order[i - 2]))
+                    for t in range(4):
+                        a(pe, ("Y", 1, 0, t, order[i - 2]))
+            a(vec, ("X", 1, 2), ("X", 1, 3))
+            a(vec, ("H", 0, 0), ("H", 0, 1))
+            a(sca, ("M", 0, 1, 0), ("M", 0, 1, 1))
+            for g in (2, 3):
+                for t in range(4):
+                    a(pe, ("Y", 1, 0, t, g))
+            for t in range(4):
+                a(vec, ("E", 1, 0, t))
+            a(sca, ("M", 1, 0, 0))
+            a(vec, ("M", 1, 0, 1), ("H", 1, 0))
+            zq = [(h, jt) for h in range(2) for jt in range(16)]
+            for i, (h, jt) in enumerate(zq):
+                place["O", h, jt] = i % 4 if i < 12 else i % 8
+            for t in range(4):
+                place["Y", 1, 1, t] = 4 + t
+            done = 0
+            for t in range(4):
+                for i in range(done, done + 2):
+                    a(pe, ("Z",) + zq[i] + (0,), ("Z",) + zq[i] + (1,))
+                done += 2
+                for g in passes[1, 1]:
+                    a(pe, ("Y", 1, 1, t, g))
+                a(vec, ("E", 1, 1, t))
+            a(vec, ("M", 1, 1, 0), ("M", 1, 1, 1), ("H", 1, 1))
+            for i in range(done, 32):
+                a(pe, ("Z",) + zq[i] + (0,), ("Z",) + zq[i] + (1,))
+            for i in range(32):
+                a(vec if i >= 12 and i % 2 else sca, ("F",) + zq[i])
+            make = {
+                "A": widen, "T": turn, "B": x_out, "X": x_quant, "C": w_mix, "W": w_quant, "K": spread, "k": spread_out,
+                "Y": mul1, "E": h_bias, "M": h_mix, "H": h_quant, "Z": mul2, "F": finish, "D": store,
+            }
+            reader = {}
+            for s in pe:
+                if s[0] == "T":
+                    reader[s] = [("B",) + s[1:]]
+                elif s[0] == "K":
+                    reader[s] = [("k",)]
+                elif s[0] == "Y" and s[4] == passes[s[1:3]][0]:
+                    reader[s] = [("E",) + s[1:4]]
+                elif s[0] == "Z" and s[3] == 0:
+                    reader[s] = [("F",) + s[1:3]]
+            needs = {}
+            last = {}
+            for s in pe:
+                n = []
+                if s in reader:
+                    if s[0] == "T":
+                        homes = [place[s]]
+                    elif s[0] == "K":
+                        homes = [5, 6, 7]
+                    elif s[0] == "Y":
+                        homes = [place[s[0:4]]]
+                    else:
+                        homes = [place[("O",) + s[1:3]]]
+                    for home in homes:
+                        n += last.get(home, [])
+                        last[home] = reader[s]
+                if s[0] == "T":
+                    n.append(("A",) + s[1:])
+                elif s[0] == "Y":
+                    n += [("W", s[4], s[2]), ("X", s[1], s[4])]
+                elif s[0] == "Z":
+                    n.append(("H", s[1], s[3]))
+                needs[s] = n
+            for q in (vec, sca):
+                mixes = [s for s in q if s[0] == "C"]
+                for s in q:
+                    n = []
+                    if s[0] == "A" and s[1] >= 2:
+                        n = [("T", s[1] - 2, g) for g in range(PASSES)]
+                    elif s[0] == "B":
+                        n = [("T",) + s[1:]] + ([("X", 0, s[2])] if s[1] >= 2 else [])
+                    elif s[0] == "X":
+                        n = [("B", 2 * s[1], s[2]), ("B", 2 * s[1] + 1, s[2])]
+                    elif s[0] == "C":
+                        i, ring = mixes.index(s), WG["V" if q is vec else "S"]
+                        n = [("W",) + mixes[i - ring][1:]] if i >= ring else []
+                    elif s[0] == "W":
+                        n = [("C",) + s[1:]]
+                    elif s[0] == "k":
+                        n = [("K",)]
+                    elif s[0] == "E":
+                        n = [("Y",) + s[1:4] + (passes[s[1:3]][-1],), ("k",)]
+                        if s[1] == 1:
+                            n.append(("M", 0, s[2], 1))
+                    elif s[0] == "M":
+                        n = [("E", s[1], s[2], t) for t in range(4)]
+                        if s[1] == 1:
+                            n.append(("H", 0, s[2]))
+                    elif s[0] == "H":
+                        n = [("M",) + s[1:3] + (k,) for k in range(2)]
+                    elif s[0] == "F":
+                        n = [("Z",) + s[1:3] + (1,), ("k",)]
+                        i = zq.index(s[1:]) // 4 - 5
+                        n += [("D",) + z for z in zq[4 * i : 4 * i + 4]] if i >= 0 else [("W", i + 5, 0), ("W", i + 5, 1)]
+                    needs[s] = n
+            sto = [("D",) + z for z in zq]
+            for s in sto:
+                needs[s] = [("F",) + s[1:]]
+            said = set()
+            queues = [["V", vec, 0], ["S", sca, 0], ["T", pe, 0], ["D", sto, 0]]
+            left = len(vec) + len(sca) + len(pe) + len(sto)
+            assert len(needs) == left, (len(needs), left)
+            while left:
+                before = left
+                for q in queues:
+                    while q[2] < len(q[1]) and all(n in said for n in needs[q[1][q[2]]]):
+                        s = q[1][q[2]]
+                        make[s[0]](q[0], *s[1:])
+                        said.add(s)
+                        q[2] += 1
+                        left -= 1
+                assert left < before, [q[1][q[2]] for q in queues if q[2] < len(q[1])]

@@ -42,9 +42,8 @@ def tile_biaffine_contact_transposed_d4_kernel(tc, x_bytes, x_scale, w, b, v, u_
         v_row = keep.tile([P, L], BF16, name="v_row")
         v_all = keep.tile([P, L], F32, name="v_all")
         b_raw = keep.tile([P, GROUPS, 4], BF16, name="b_raw")
-        b_col = keep.tile([P, GROUPS, 4], F32, name="b_col")
-        c_raw = keep.tile([16, P], BF16, name="c_raw")
-        c_row = keep.tile([P, P], F32, name="c_row")
+        c_row = keep.tile([P, P], BF16, name="c_row")
+        ident_h = keep.tile([P, P], BF16, name="ident_h")
         c_col = keep.tile([P, 16], F32, name="c_col")
         x_codes = keep.tile([P, PASSES, L], U32, name="x_codes", align_bytes=64)
         x_planes = keep.tile([P, PASSES, L], U8, name="x_planes", align_bytes=64)
@@ -57,8 +56,9 @@ def tile_biaffine_contact_transposed_d4_kernel(tc, x_bytes, x_scale, w, b, v, u_
 
         with tc.manual_schedule():
             make_identity(nc, ident[:])
-            nc.gpsimd.memset(v_row[:], 0.0)
-            nc.gpsimd.memset(c_row[:], 0.0)
+            nc.vector.memset(v_row[:], 0.0)
+            nc.vector.memset(c_row[:], 0.0)
+            nc.vector.tensor_copy(out=ident_h[:], in_=ident[:])
             nc.gpsimd.memset(ones[:], 1.0)
             nc.gpsimd.memset(u_s[:].rearrange("p g n -> p (g n)").bitcast(I32), 0)
 
@@ -78,11 +78,9 @@ def tile_biaffine_contact_transposed_d4_kernel(tc, x_bytes, x_scale, w, b, v, u_
 
             for r in range(4):
                 load_x(r)
-            nc.gpsimd.dma_start(out=v_row[0:1, :], in_=v.rearrange("(o i) -> o i", o=1))
-            nc.gpsimd.dma_start(out=c_raw[:], in_=c.rearrange("(j p) -> j p", p=P))
-            nc.gpsimd.dma_start(out=b_raw[:], in_=b.rearrange("(g p t) -> p g t", p=P, t=4))
-            nc.gpsimd.tensor_copy(out=c_row[0:16, :], in_=c_raw[:])
-            nc.gpsimd.tensor_copy(out=b_col[:], in_=b_raw[:])
+            nc.sync.dma_start(out=v_row[0:1, :], in_=v.rearrange("(o i) -> o i", o=1))
+            nc.sync.dma_start(out=c_row[0:16, :], in_=c.rearrange("(j p) -> j p", p=P))
+            nc.sync.dma_start(out=b_raw[:], in_=b.rearrange("(g p t) -> p g t", p=P, t=4))
             for g in range(PASSES):
                 load_w(g)
             for r in range(4, 8):
@@ -96,7 +94,9 @@ def tile_biaffine_contact_transposed_d4_kernel(tc, x_bytes, x_scale, w, b, v, u_
                 )
 
             xw, xg, wg, hs, hg, o_tile = {}, {}, {}, {}, {}, {}
-            bank_of = {}
+            bank_of, bank_now = {}, {}
+            wide = (512, 256, 256)
+            span = (slice(0, 512), slice(512, 768), slice(768, 1024))
             wg_count = {"V": 0, "S": 0}
 
             def widen(eng, pair, g):
@@ -134,21 +134,22 @@ def tile_biaffine_contact_transposed_d4_kernel(tc, x_bytes, x_scale, w, b, v, u_
                         nc.tensor.transpose(tv[:, u, P * k : P * k + P], words, ident[:])
 
             def x_out(eng, pair, g):
-                h, k = pair // 2, pair % 2
-                if (h, g) not in xg:
-                    xg[h, g] = work.tile([P, HALF, 4], BF16, name="xg%d" % g, bufs=1, align_bytes=64)
-                dst = xg[h, g][:, 256 * k : 256 * k + 256, :].rearrange("p r j -> p (r j)").bitcast(F32).rearrange("p (r u) -> p r u", u=2)
+                ch = max(0, pair - 1)
+                k, n = (pair, 2) if ch == 0 else (0, 1)
+                if (ch, g) not in xg:
+                    xg[ch, g] = work.tile([P, 256 * n, 4], BF16, name="xg%d" % g, bufs=1, align_bytes=64)
+                dst = xg[ch, g][:, 256 * k : 256 * k + 256, :].rearrange("p r j -> p (r j)").bitcast(F32).rearrange("p (r u) -> p r u", u=2)
                 src = bank_of["T", pair, g][:].rearrange("p (u r) -> p r u", u=2)
                 if eng == "S":
                     nc.scalar.copy(out=dst, in_=src)
                 else:
                     nc.vector.tensor_copy(out=dst, in_=src)
 
-            def x_quant(eng, h, g):
+            def x_quant(eng, ch, g):
                 nc.vector.quantize_mx(
-                    out=x_codes[:, g, HALF * h : HALF * h + HALF].bitcast(E4M3X4),
-                    scales=x_planes[:, g, HALF * h : HALF * h + HALF],
-                    in_=xg[h, g][:].rearrange("p r j -> p (r j)"),
+                    out=x_codes[:, g, span[ch]].bitcast(E4M3X4),
+                    scales=x_planes[:, g, span[ch]],
+                    in_=xg[ch, g][:].rearrange("p r j -> p (r j)"),
                 )
 
             def w_mix(eng, g, G):
@@ -169,71 +170,62 @@ def tile_biaffine_contact_transposed_d4_kernel(tc, x_bytes, x_scale, w, b, v, u_
                 )
 
             def spread(eng):
-                bank_of["v0"], bank_of["v1"], bank_of["c"] = bank(6), bank(7), bank(5)
+                bank_of["v0"], bank_of["v1"], bank_of["c"] = bank(6), bank(7), psum.tile([P, 2 * HALF], BF16, name="bank5")
                 for k in range(2):
                     nc.tensor.matmul(bank_of["v%d" % k][:], lhsT=ones[:], rhs=v_row[:, 512 * k : 512 * k + 512], start=True, stop=True)
-                nc.tensor.transpose(bank_of["c"][:, 0:P], c_row[:], ident[:])
+                nc.tensor.transpose(bank_of["c"][:, 0:P], c_row[:], ident_h[:])
 
             def spread_out(eng):
                 for k in range(2):
                     nc.scalar.copy(out=v_all[:, 512 * k : 512 * k + 512], in_=bank_of["v%d" % k][:])
                 nc.scalar.copy(out=c_col[:], in_=bank_of["c"][:, 0:16])
 
-            def mul1(eng, h, G, t, g):
-                if g == passes[h, G][0]:
-                    bank_of[h, G, t] = bank(place["Y", h, G, t])
-                col = 512 * G + P * t
+            def mul1(eng, ch, G, t, g):
+                home, col = place["Y", ch, G, t]
+                if g == passes[ch, G][0]:
+                    if col == 0:
+                        bank_now[home] = bank(home)
+                    bank_of["Y", ch, G, t] = bank_now[home][:, col : col + wide[ch]]
+                f = 512 * G + P * t
                 nc.tensor.matmul_mx(
-                    out=bank_of[h, G, t][:],
-                    lhsT=w_codes[:, g, col : col + P].bitcast(E4M3X4),
-                    lhsT_scale=w_planes[:, g, col : col + P],
-                    rhs=x_codes[:, g, HALF * h : HALF * h + HALF].bitcast(E4M3X4),
-                    rhs_scale=x_planes[:, g, HALF * h : HALF * h + HALF],
-                    start=(g == passes[h, G][0]),
-                    stop=(g == passes[h, G][-1]),
+                    out=bank_of["Y", ch, G, t],
+                    lhsT=w_codes[:, g, f : f + P].bitcast(E4M3X4),
+                    lhsT_scale=w_planes[:, g, f : f + P],
+                    rhs=x_codes[:, g, span[ch]].bitcast(E4M3X4),
+                    rhs_scale=x_planes[:, g, span[ch]],
+                    start=(g == passes[ch, G][0]),
+                    stop=(g == passes[ch, G][-1]),
                 )
 
-            def h_bias(eng, h, G, t):
-                if eng == "S":
-                    if t == 0:
-                        hs[h, G] = work.tile([P, 4, HALF], F32, name="hs", bufs=2)
-                    nc.scalar.activation(out=hs[h, G][:, t, :], in_=bank_of[h, G, t][:], func=IDENT, bias=b_col[:, G, t : t + 1], scale=1.0)
-                else:
-                    if t == 0:
-                        hs[h, G] = work.tile([P, 4, HALF], BF16, name="hb", bufs=2)
-                    nc.vector.scalar_tensor_tensor(
-                        out=hs[h, G][:, t, :],
-                        in0=bank_of[h, G, t][:],
-                        scalar=b_col[:, G, t : t + 1],
-                        in1=v_all[:, HALF * h : HALF * h + HALF],
-                        op0=ADD,
-                        op1=MULT,
-                    )
-
-            def h_mix(eng, h, G, k):
-                s = HALF // 2
-                if (h, G) not in hg:
-                    hg[h, G] = work.tile([P, HALF, 4], BF16, name="hg", bufs=2, align_bytes=64)
-                dst = hg[h, G][:, s * k : s * k + s, :]
-                src = hs[h, G][:, :, s * k : s * k + s].rearrange("p t i -> p i t")
-                if ("E", h, G, 0) not in on_s:
-                    if eng == "S":
-                        nc.scalar.copy(out=dst, in_=src)
+            def h_bias(eng, ch, G, t):
+                if (ch, G) not in hs:
+                    if ch == 0:
+                        hs[ch, G] = work.tile([P, 4, HALF], F32, name="hs%d" % G, bufs=1)
                     else:
-                        nc.vector.tensor_copy(out=dst, in_=src)
+                        hs[ch, G] = work.tile([P, 4, HALF], F32, name="wr%d" % (2 + ch), bufs=1) if G == 0 else hs[ch, 0]
+                dst = hs[ch, G][:, t, 256 * G * (ch > 0) : 256 * G * (ch > 0) + wide[ch]]
+                if eng == "S":
+                    nc.scalar.activation(out=dst, in_=bank_of["Y", ch, G, t], func=IDENT, bias=b_raw[:, G, t : t + 1], scale=1.0)
                 else:
-                    nc.vector.tensor_tensor(
-                        out=dst,
-                        in0=src,
-                        in1=v_all[:, HALF * h + s * k : HALF * h + s * k + s].unsqueeze(2).to_broadcast([P, s, 4]),
-                        op=MULT,
-                    )
+                    nc.vector.tensor_scalar(out=dst, in0=bank_of["Y", ch, G, t], scalar1=b_raw[:, G, t : t + 1], scalar2=None, op0=ADD)
 
-            def h_quant(eng, h, G):
+            def h_mix(eng, ch, G, k):
+                if (ch, G) not in hg:
+                    hg[ch, G] = work.tile([P, wide[ch], 4], BF16, name="hg%d" % G, bufs=1, align_bytes=64)
+                c0 = 256 * G * (ch > 0) + 256 * k
+                i0 = span[ch].start + 256 * k
+                nc.vector.tensor_tensor(
+                    out=hg[ch, G][:, 256 * k : 256 * k + 256, :],
+                    in0=hs[ch, G][:, :, c0 : c0 + 256].rearrange("p t i -> p i t"),
+                    in1=v_all[:, i0 : i0 + 256].unsqueeze(2).to_broadcast([P, 256, 4]),
+                    op=MULT,
+                )
+
+            def h_quant(eng, ch, G):
                 nc.vector.quantize_mx(
-                    out=h_codes[:, G, HALF * h : HALF * h + HALF].bitcast(E4M3X4),
-                    scales=h_planes[:, G, HALF * h : HALF * h + HALF],
-                    in_=hg[h, G][:].rearrange("p i t -> p (i t)"),
+                    out=h_codes[:, G, span[ch]].bitcast(E4M3X4),
+                    scales=h_planes[:, G, span[ch]],
+                    in_=hg[ch, G][:].rearrange("p i t -> p (i t)"),
                 )
 
             def mul2(eng, h, jt, G):
@@ -252,7 +244,7 @@ def tile_biaffine_contact_transposed_d4_kernel(tc, x_bytes, x_scale, w, b, v, u_
             def finish(eng, h, jt):
                 i = zq.index((h, jt))
                 if i // 4 not in o_tile:
-                    o_tile[i // 4] = work.tile([P, 4, HALF], F32, name="wr%d" % (i // 4 % 5), bufs=1)
+                    o_tile[i // 4] = work.tile([P, 4, HALF], F32, name="wr%d" % (i // 4 % 3), bufs=1)
                 t = o_tile[i // 4][:, i % 4, :]
                 if eng == "S":
                     nc.scalar.activation(out=t, in_=bank_of["O", h, jt][:], func=IDENT, bias=c_col[:, jt : jt + 1], scale=1.0)
@@ -263,10 +255,9 @@ def tile_biaffine_contact_transposed_d4_kernel(tc, x_bytes, x_scale, w, b, v, u_
                 nc.sync.dma_start(out=out[P * jt : P * jt + P, HALF * h : HALF * h + HALF], in_=o_tile[zq.index((h, jt)) // 4][:, zq.index((h, jt)) % 4, :])
 
             vec, sca, pe, place = [], [], [], {}
-            on_s = {("A", pair, 4) for pair in range(4)}
-            passes = {(h, G): (0, 1, 2, 3, 4) for h in range(2) for G in range(2)}
+            on_s = {("A", 0, 4), ("A", 1, 4)}
+            passes = {(ch, G): (0, 1, 2, 3, 4) for ch in range(3) for G in range(2)}
             passes[0, 1] = (0, 3, 1, 4, 2)
-            passes[1, 0] = passes[1, 1] = (4, 0, 1, 2, 3)
 
             def a(q, *ss):
                 q.extend(ss)
@@ -286,70 +277,73 @@ def tile_biaffine_contact_transposed_d4_kernel(tc, x_bytes, x_scale, w, b, v, u_
             a(sca, ("B", 0, 2), ("B", 0, 3), ("B", 0, 4))
             for g in range(5):
                 a(sca, ("B", 1, g))
-            a(pe, ("K",))
+            last = []
             a(vec, ("C", 0, 0), ("X", 0, 0), ("X", 0, 1), ("W", 0, 0), ("X", 0, 2), ("C", 2, 0), ("W", 1, 0), ("X", 0, 3), ("X", 0, 4), ("W", 2, 0))
             a(sca, ("C", 1, 0), ("C", 0, 1), ("C", 3, 0), ("k",))
             a(vec, ("W", 0, 1), ("C", 4, 0), ("W", 3, 0), ("W", 4, 0))
             a(sca, ("C", 1, 1), ("C", 2, 1))
             a(vec, ("C", 3, 1), ("C", 4, 1), ("W", 3, 1), ("W", 1, 1), ("W", 4, 1))
-            for t in range(4):
-                a(vec, ("E", 0, 0, t))
             a(vec, ("W", 2, 1))
             for G in range(2):
-                for g in passes[0, G]:
+                for i, g in enumerate(passes[0, G]):
                     for t in range(4):
-                        a(pe, ("Y", 0, G, t, g))
-            for G in range(2):
-                for t in range(4):
-                    place["Y", 0, G, t] = 4 * G + t
-                    place["Y", 1, G, t] = 4 * (1 - G) + t
-            a(sca, ("A", 2, 4), ("A", 3, 4))
-            a(sca, ("M", 0, 0, 0), ("M", 0, 0, 1))
-            n = 0
-            order = (4, 0, 1, 2, 3)
-            for i, g in enumerate(order):
-                for pair in (2, 3):
-                    if g != 4:
-                        a(vec, ("A", pair, g))
-                    a(pe, ("T", pair, g))
-                    place["T", pair, g] = n % 4
-                    a(sca, ("B", pair, g))
-                    n += 1
-                if i == 2:
-                    for t in range(4):
-                        a(vec, ("E", 0, 1, t))
-                if i >= 2:
-                    a(vec, ("X", 1, order[i - 2]))
-                    for t in range(4):
-                        a(pe, ("Y", 1, 0, t, order[i - 2]))
-            a(vec, ("X", 1, 2), ("X", 1, 3))
-            a(vec, ("H", 0, 0), ("H", 0, 1))
-            a(sca, ("M", 0, 1, 0), ("M", 0, 1, 1))
-            for g in (2, 3):
-                for t in range(4):
-                    a(pe, ("Y", 1, 0, t, g))
-            for t in range(4):
-                a(vec, ("E", 1, 0, t))
-            a(sca, ("M", 1, 0, 0))
-            a(vec, ("M", 1, 0, 1), ("H", 1, 0))
+                        a(last if (G, i) == (1, 4) else pe, ("Y", 0, G, t, g))
+                        place["Y", 0, G, t] = (4 * G + t, 0)
+                    if G == 0 and i == 1:
+                        a(pe, ("K",))
             zq = [(h, jt) for h in range(2) for jt in range(16)]
-            for i, (h, jt) in enumerate(zq):
-                place["O", h, jt] = i % 4 if i < 12 else i % 8
-            for t in range(4):
-                place["Y", 1, 1, t] = 4 + t
-            done = 0
-            for t in range(4):
-                for i in range(done, done + 2):
+            nz = 0
+
+            def z(n, homes):
+                for i in range(nz, nz + n):
+                    place[("O",) + zq[i]] = homes[i % len(homes)]
                     a(pe, ("Z",) + zq[i] + (0,), ("Z",) + zq[i] + (1,))
-                done += 2
-                for g in passes[1, 1]:
-                    a(pe, ("Y", 1, 1, t, g))
-                a(vec, ("E", 1, 1, t))
-            a(vec, ("M", 1, 1, 0), ("M", 1, 1, 1), ("H", 1, 1))
-            for i in range(done, 32):
-                a(pe, ("Z",) + zq[i] + (0,), ("Z",) + zq[i] + (1,))
-            for i in range(32):
-                a(vec if i >= 12 and i % 2 else sca, ("F",) + zq[i])
+                return nz + n
+
+            def f(lo, hi, eng):
+                for i in range(lo, hi):
+                    a(vec if eng[i % len(eng)] == "V" else sca, ("F",) + zq[i])
+
+            for t in range(4):
+                a(sca, ("E", 0, 0, t))
+            for i in range(10):
+                place["T", 2 + i // 5, i % 5] = i % 2
+            for g in range(5):
+                a(vec, ("A", 2, g))
+                a(pe, ("T", 2, g))
+                if g == 1:
+                    a(pe, *last)
+                a(sca, ("B", 2, g))
+            for t in range(4):
+                a(sca, ("E", 0, 1, t))
+            a(vec, ("X", 1, 0), ("X", 1, 1), ("A", 3, 0), ("X", 1, 2), ("A", 3, 1), ("X", 1, 3), ("X", 1, 4))
+            a(vec, ("A", 3, 2), ("A", 3, 3), ("A", 3, 4), ("M", 0, 0, 0), ("X", 2, 0), ("X", 2, 1), ("M", 0, 0, 1), ("X", 2, 2), ("X", 2, 3), ("H", 0, 0), ("M", 0, 1, 0), ("X", 2, 4), ("M", 0, 1, 1), ("H", 0, 1))
+
+            def y256(ch, G, homes, turns=()):
+                turns = list(turns)
+                for t0 in (0, 2):
+                    for g in passes[ch, G]:
+                        for t in (t0, t0 + 1):
+                            a(pe, ("Y", ch, G, t, g))
+                    for n in turns[t0 : t0 + 2]:
+                        a(pe, ("T", 3, n))
+                        a(sca, ("B", 3, n))
+                    for t in (t0, t0 + 1):
+                        a(sca, ("E", ch, G, t))
+                for t in range(4):
+                    place["Y", ch, G, t] = (homes[t % 2], 256 * (t // 2))
+
+            y256(1, 0, (2, 3), (0, 1, 2, 3))
+            y256(1, 1, (4, 5), (4,))
+            y256(2, 0, (2, 3))
+            y256(2, 1, (4, 5))
+            nz = z(4, (6, 7, 0, 1))
+            for ch in (1, 2):
+                for G in range(2):
+                    a(vec, ("M", ch, G, 0), ("H", ch, G))
+            nz = z(28, (6, 7, 0, 1, 2, 3, 4, 5))
+            f(0, 13, "S")
+            f(13, 32, "SV")
             make = {
                 "A": widen, "T": turn, "B": x_out, "X": x_quant, "C": w_mix, "W": w_quant, "K": spread, "k": spread_out,
                 "Y": mul1, "E": h_bias, "M": h_mix, "H": h_quant, "Z": mul2, "F": finish, "D": store,
@@ -374,18 +368,21 @@ def tile_biaffine_contact_transposed_d4_kernel(tc, x_bytes, x_scale, w, b, v, u_
                     elif s[0] == "K":
                         homes = [5, 6, 7]
                     elif s[0] == "Y":
-                        homes = [place[s[0:4]]]
+                        homes = [place[s[0:4]][0]]
                     else:
                         homes = [place[("O",) + s[1:3]]]
                     for home in homes:
-                        n += last.get(home, [])
-                        last[home] = reader[s]
+                        if s[0] == "Y" and place[s[0:4]][1]:
+                            last[home] = last[home] + reader[s]
+                        else:
+                            n += last.get(home, [])
+                            last[home] = reader[s]
                 if s[0] == "T":
                     n.append(("A",) + s[1:])
                 elif s[0] == "Y":
                     n += [("W", s[4], s[2]), ("X", s[1], s[4])]
                 elif s[0] == "Z":
-                    n.append(("H", s[1], s[3]))
+                    n += [("H", ch, s[3]) for ch in ((0,) if s[1] == 0 else (1, 2))]
                 needs[s] = n
             for q in (vec, sca):
                 mixes = [s for s in q if s[0] == "C"]
@@ -394,9 +391,9 @@ def tile_biaffine_contact_transposed_d4_kernel(tc, x_bytes, x_scale, w, b, v, u_
                     if s[0] == "A" and s[1] >= 2:
                         n = [("T", s[1] - 2, g) for g in range(PASSES)]
                     elif s[0] == "B":
-                        n = [("T",) + s[1:]] + ([("X", 0, s[2])] if s[1] >= 2 else [])
+                        n = [("T",) + s[1:]] + ([("X", s[1] - 2, s[2])] if s[1] >= 2 else [])
                     elif s[0] == "X":
-                        n = [("B", 2 * s[1], s[2]), ("B", 2 * s[1] + 1, s[2])]
+                        n = [("B", s[1] + 1, s[2])] + ([("B", 0, s[2])] if s[1] == 0 else [])
                     elif s[0] == "C":
                         i, ring = mixes.index(s), WG["V" if q is vec else "S"]
                         n = [("W",) + mixes[i - ring][1:]] if i >= ring else []
@@ -406,18 +403,18 @@ def tile_biaffine_contact_transposed_d4_kernel(tc, x_bytes, x_scale, w, b, v, u_
                         n = [("K",)]
                     elif s[0] == "E":
                         n = [("Y",) + s[1:4] + (passes[s[1:3]][-1],), ("k",)]
-                        if s[1] == 1:
-                            n.append(("M", 0, s[2], 1))
+                        if s[1] > 0:
+                            n += [("W", 2 + s[1], 0), ("W", 2 + s[1], 1)]
                     elif s[0] == "M":
                         n = [("E", s[1], s[2], t) for t in range(4)]
-                        if s[1] == 1:
-                            n.append(("H", 0, s[2]))
+                        if s[1] > 0:
+                            n.append(("H", s[1] - 1, s[2]))
                     elif s[0] == "H":
-                        n = [("M",) + s[1:3] + (k,) for k in range(2)]
+                        n = [("M",) + s[1:3] + (k,) for k in range(2 if s[1] == 0 else 1)]
                     elif s[0] == "F":
                         n = [("Z",) + s[1:3] + (1,), ("k",)]
-                        i = zq.index(s[1:]) // 4 - 5
-                        n += [("D",) + z for z in zq[4 * i : 4 * i + 4]] if i >= 0 else [("W", i + 5, 0), ("W", i + 5, 1)]
+                        i = zq.index(s[1:]) // 4 - 3
+                        n += [("D",) + z for z in zq[4 * i : 4 * i + 4]] if i >= 0 else [("W", i + 3, 0), ("W", i + 3, 1)]
                     needs[s] = n
             sto = [("D",) + z for z in zq]
             for s in sto:

@@ -38,9 +38,7 @@ def tile_biaffine_contact_transposed_d4_kernel(tc, x_bytes, x_scale, w, b, v, u_
 
         x_sc = keep.tile([P, 8, 20], F32, name="x_sc")
         ident = keep.tile([P, P], F32, name="ident")
-        ones = keep.tile([P, P], BF16, name="ones")
-        v_row = keep.tile([P, L], BF16, name="v_row")
-        v_all = keep.tile([P, L], F32, name="v_all")
+        v_all = keep.tile([P, L], BF16, name="v_all")
         b_raw = keep.tile([P, GROUPS, 4], BF16, name="b_raw")
         c_row = keep.tile([P, P], BF16, name="c_row")
         ident_h = keep.tile([P, P], BF16, name="ident_h")
@@ -56,10 +54,8 @@ def tile_biaffine_contact_transposed_d4_kernel(tc, x_bytes, x_scale, w, b, v, u_
 
         with tc.manual_schedule():
             make_identity(nc, ident[:])
-            nc.vector.memset(v_row[:], 0.0)
             nc.vector.memset(c_row[:], 0.0)
             nc.vector.tensor_copy(out=ident_h[:], in_=ident[:])
-            nc.gpsimd.memset(ones[:], 1.0)
             nc.gpsimd.memset(u_s[:].rearrange("p g n -> p (g n)").bitcast(I32), 0)
 
             nc.scalar.dma_start(out=x_sc[:], in_=x_scale.rearrange("(r p) d -> p r d", p=P))
@@ -78,13 +74,12 @@ def tile_biaffine_contact_transposed_d4_kernel(tc, x_bytes, x_scale, w, b, v, u_
 
             for r in range(4):
                 load_x(r)
-            nc.sync.dma_start(out=v_row[0:1, :], in_=v.rearrange("(o i) -> o i", o=1))
-            nc.sync.dma_start(out=c_row[0:16, :], in_=c.rearrange("(j p) -> j p", p=P))
-            nc.sync.dma_start(out=b_raw[:], in_=b.rearrange("(g p t) -> p g t", p=P, t=4))
             for g in range(PASSES):
                 load_w(g)
             for r in range(4, 8):
                 load_x(r)
+            nc.sync.dma_start(out=b_raw[:], in_=b.rearrange("(g p t) -> p g t", p=P, t=4))
+            nc.sync.dma_start(out=c_row[0:16, :], in_=c.rearrange("(j p) -> j p", p=P))
             for g in range(GROUPS):
                 nc.sync.dma_start(out=u_w[:, g, :].bitcast(I32), in_=u_words[g].bitcast(I32))
             for q in range(4):
@@ -92,6 +87,7 @@ def tile_biaffine_contact_transposed_d4_kernel(tc, x_bytes, x_scale, w, b, v, u_
                     out=u_s[32 * q : 32 * q + 4, :, :].bitcast(I32),
                     in_=u_scales[:, 4 * q : 4 * q + 4, :].rearrange("g q n -> q g n").bitcast(I32),
                 )
+            nc.sync.dma_start(out=v_all[:], in_=v.partition_broadcast(128))
 
             xw, xg, wg, hs, hg, o_tile = {}, {}, {}, {}, {}, {}
             bank_of, bank_now = {}, {}
@@ -156,11 +152,12 @@ def tile_biaffine_contact_transposed_d4_kernel(tc, x_bytes, x_scale, w, b, v, u_
                 t = work.tile([P, 4, P, 4], BF16, name="wg%s%d" % (eng, wg_count[eng] % WG[eng]), bufs=1, align_bytes=64)
                 wg_count[eng] += 1
                 wg[g, G] = t
-                src = wr[g][:, :, 512 * G : 512 * G + 512].rearrange("p j (m t) -> p t m j", t=4)
+                dst = t[:].rearrange("p t m j -> p m j t")
+                src = wr[g][:, :, 512 * G : 512 * G + 512].rearrange("p j (m t) -> p m j t", t=4)
                 if eng == "S":
-                    nc.scalar.copy(out=t[:], in_=src)
+                    nc.scalar.copy(out=dst, in_=src)
                 else:
-                    nc.vector.tensor_copy(out=t[:], in_=src)
+                    nc.vector.tensor_copy(out=dst, in_=src)
 
             def w_quant(eng, g, G):
                 nc.vector.quantize_mx(
@@ -170,14 +167,10 @@ def tile_biaffine_contact_transposed_d4_kernel(tc, x_bytes, x_scale, w, b, v, u_
                 )
 
             def spread(eng):
-                bank_of["v0"], bank_of["v1"], bank_of["c"] = bank(6), bank(7), psum.tile([P, 2 * HALF], BF16, name="bank5")
-                for k in range(2):
-                    nc.tensor.matmul(bank_of["v%d" % k][:], lhsT=ones[:], rhs=v_row[:, 512 * k : 512 * k + 512], start=True, stop=True)
+                bank_of["c"] = psum.tile([P, 2 * HALF], BF16, name="bank1")
                 nc.tensor.transpose(bank_of["c"][:, 0:P], c_row[:], ident_h[:])
 
             def spread_out(eng):
-                for k in range(2):
-                    nc.scalar.copy(out=v_all[:, 512 * k : 512 * k + 512], in_=bank_of["v%d" % k][:])
                 nc.scalar.copy(out=c_col[:], in_=bank_of["c"][:, 0:16])
 
             def mul1(eng, ch, G, t, g):
@@ -198,28 +191,47 @@ def tile_biaffine_contact_transposed_d4_kernel(tc, x_bytes, x_scale, w, b, v, u_
                 )
 
             def h_bias(eng, ch, G, t):
+                split = ("E", ch, G, 0) in on_s
                 if (ch, G) not in hs:
-                    if ch == 0:
-                        hs[ch, G] = work.tile([P, 4, HALF], F32, name="hs%d" % G, bufs=1)
+                    name = "hs%d" % G if ch == 0 else "wr%d" % (2 + ch)
+                    if ch == 0 or G == 0:
+                        hs[ch, G] = work.tile([P, 4, HALF], F32 if split else BF16, name=name, bufs=1)
                     else:
-                        hs[ch, G] = work.tile([P, 4, HALF], F32, name="wr%d" % (2 + ch), bufs=1) if G == 0 else hs[ch, 0]
+                        hs[ch, G] = hs[ch, 0]
                 dst = hs[ch, G][:, t, 256 * G * (ch > 0) : 256 * G * (ch > 0) + wide[ch]]
-                if eng == "S":
+                if split:
                     nc.scalar.activation(out=dst, in_=bank_of["Y", ch, G, t], func=IDENT, bias=b_raw[:, G, t : t + 1], scale=1.0)
                 else:
-                    nc.vector.tensor_scalar(out=dst, in0=bank_of["Y", ch, G, t], scalar1=b_raw[:, G, t : t + 1], scalar2=None, op0=ADD)
+                    nc.vector.scalar_tensor_tensor(
+                        out=dst,
+                        in0=bank_of["Y", ch, G, t],
+                        scalar=b_raw[:, G, t : t + 1],
+                        in1=v_all[:, span[ch]],
+                        op0=ADD,
+                        op1=MULT,
+                    )
 
             def h_mix(eng, ch, G, k):
                 if (ch, G) not in hg:
                     hg[ch, G] = work.tile([P, wide[ch], 4], BF16, name="hg%d" % G, bufs=1, align_bytes=64)
                 c0 = 256 * G * (ch > 0) + 256 * k
                 i0 = span[ch].start + 256 * k
-                nc.vector.tensor_tensor(
-                    out=hg[ch, G][:, 256 * k : 256 * k + 256, :],
-                    in0=hs[ch, G][:, :, c0 : c0 + 256].rearrange("p t i -> p i t"),
-                    in1=v_all[:, i0 : i0 + 256].unsqueeze(2).to_broadcast([P, 256, 4]),
-                    op=MULT,
-                )
+                dst = hg[ch, G][:, 256 * k : 256 * k + 256, :]
+                src = hs[ch, G][:, :, c0 : c0 + 256]
+                if ("E", ch, G, 0) in on_s:
+                    nc.vector.tensor_tensor(
+                        out=dst,
+                        in0=src.rearrange("p t i -> p i t"),
+                        in1=v_all[:, i0 : i0 + 256].unsqueeze(2).to_broadcast([P, 256, 4]),
+                        op=MULT,
+                    )
+                else:
+                    dst = dst.rearrange("p (c i) t -> p c t i", i=4)
+                    src = src.rearrange("p t (c i) -> p c t i", i=4)
+                    if eng == "S":
+                        nc.scalar.copy(out=dst, in_=src)
+                    else:
+                        nc.vector.tensor_copy(out=dst, in_=src)
 
             def h_quant(eng, ch, G):
                 nc.vector.quantize_mx(
@@ -256,6 +268,7 @@ def tile_biaffine_contact_transposed_d4_kernel(tc, x_bytes, x_scale, w, b, v, u_
 
             vec, sca, pe, place = [], [], [], {}
             on_s = {("A", 0, 4), ("A", 1, 4)}
+            on_s |= {("E", ch, G, 0) for ch in range(3) for G in range(2)}
             passes = {(ch, G): (0, 1, 2, 3, 4) for ch in range(3) for G in range(2)}
             passes[0, 1] = (0, 3, 1, 4, 2)
 
@@ -279,7 +292,7 @@ def tile_biaffine_contact_transposed_d4_kernel(tc, x_bytes, x_scale, w, b, v, u_
                 a(sca, ("B", 1, g))
             last = []
             a(vec, ("C", 0, 0), ("X", 0, 0), ("X", 0, 1), ("W", 0, 0), ("X", 0, 2), ("C", 2, 0), ("W", 1, 0), ("X", 0, 3), ("X", 0, 4), ("W", 2, 0))
-            a(sca, ("C", 1, 0), ("C", 0, 1), ("C", 3, 0), ("k",))
+            a(sca, ("C", 1, 0), ("C", 0, 1), ("C", 3, 0))
             a(vec, ("W", 0, 1), ("C", 4, 0), ("W", 3, 0), ("W", 4, 0))
             a(sca, ("C", 1, 1), ("C", 2, 1))
             a(vec, ("C", 3, 1), ("C", 4, 1), ("W", 3, 1), ("W", 1, 1), ("W", 4, 1))
@@ -289,8 +302,6 @@ def tile_biaffine_contact_transposed_d4_kernel(tc, x_bytes, x_scale, w, b, v, u_
                     for t in range(4):
                         a(last if (G, i) == (1, 4) else pe, ("Y", 0, G, t, g))
                         place["Y", 0, G, t] = (4 * G + t, 0)
-                    if G == 0 and i == 1:
-                        a(pe, ("K",))
             zq = [(h, jt) for h in range(2) for jt in range(16)]
             nz = 0
 
@@ -307,17 +318,20 @@ def tile_biaffine_contact_transposed_d4_kernel(tc, x_bytes, x_scale, w, b, v, u_
             for t in range(4):
                 a(sca, ("E", 0, 0, t))
             for i in range(10):
-                place["T", 2 + i // 5, i % 5] = i % 2
+                place["T", 2 + i // 5, i % 5] = (0, 1, 2, 3, 0, 1, 0, 1, 0, 1)[i]
             for g in range(5):
                 a(vec, ("A", 2, g))
                 a(pe, ("T", 2, g))
                 if g == 1:
                     a(pe, *last)
                 a(sca, ("B", 2, g))
+            a(sca, ("k",))
             for t in range(4):
                 a(sca, ("E", 0, 1, t))
-            a(vec, ("X", 1, 0), ("X", 1, 1), ("A", 3, 0), ("X", 1, 2), ("A", 3, 1), ("X", 1, 3), ("X", 1, 4))
-            a(vec, ("A", 3, 2), ("A", 3, 3), ("A", 3, 4), ("M", 0, 0, 0), ("X", 2, 0), ("X", 2, 1), ("M", 0, 0, 1), ("X", 2, 2), ("X", 2, 3), ("H", 0, 0), ("M", 0, 1, 0), ("X", 2, 4), ("M", 0, 1, 1), ("H", 0, 1))
+            a(vec, ("X", 1, 0), ("X", 1, 1), ("A", 3, 0), ("X", 1, 2), ("X", 1, 3), ("A", 3, 1), ("X", 1, 4))
+            a(vec, ("A", 3, 2), ("A", 3, 3), ("A", 3, 4), ("M", 0, 0, 0), ("X", 2, 0), ("X", 2, 1), ("M", 0, 0, 1), ("X", 2, 2), ("X", 2, 3), ("X", 2, 4), ("H", 0, 0), ("M", 0, 1, 0), ("M", 0, 1, 1), ("H", 0, 1))
+
+            a(pe, ("K",))
 
             def y256(ch, G, homes, turns=()):
                 turns = list(turns)
@@ -325,7 +339,7 @@ def tile_biaffine_contact_transposed_d4_kernel(tc, x_bytes, x_scale, w, b, v, u_
                     for g in passes[ch, G]:
                         for t in (t0, t0 + 1):
                             a(pe, ("Y", ch, G, t, g))
-                    for n in turns[t0 : t0 + 2]:
+                    for n in turns[t0 : t0 + 2] if t0 == 0 else turns[2:]:
                         a(pe, ("T", 3, n))
                         a(sca, ("B", 3, n))
                     for t in (t0, t0 + 1):
@@ -333,8 +347,8 @@ def tile_biaffine_contact_transposed_d4_kernel(tc, x_bytes, x_scale, w, b, v, u_
                 for t in range(4):
                     place["Y", ch, G, t] = (homes[t % 2], 256 * (t // 2))
 
-            y256(1, 0, (2, 3), (0, 1, 2, 3))
-            y256(1, 1, (4, 5), (4,))
+            y256(1, 0, (2, 3), (0, 1, 2, 3, 4))
+            y256(1, 1, (4, 5))
             y256(2, 0, (2, 3))
             y256(2, 1, (4, 5))
             nz = z(4, (6, 7, 0, 1))
@@ -366,7 +380,7 @@ def tile_biaffine_contact_transposed_d4_kernel(tc, x_bytes, x_scale, w, b, v, u_
                     if s[0] == "T":
                         homes = [place[s]]
                     elif s[0] == "K":
-                        homes = [5, 6, 7]
+                        homes = [1]
                     elif s[0] == "Y":
                         homes = [place[s[0:4]][0]]
                     else:
@@ -402,7 +416,7 @@ def tile_biaffine_contact_transposed_d4_kernel(tc, x_bytes, x_scale, w, b, v, u_
                     elif s[0] == "k":
                         n = [("K",)]
                     elif s[0] == "E":
-                        n = [("Y",) + s[1:4] + (passes[s[1:3]][-1],), ("k",)]
+                        n = [("Y",) + s[1:4] + (passes[s[1:3]][-1],)]
                         if s[1] > 0:
                             n += [("W", 2 + s[1], 0), ("W", 2 + s[1], 1)]
                     elif s[0] == "M":

@@ -58,7 +58,8 @@ def tile_biaffine_contact_transposed_d4_kernel(tc, x_bytes, x_scale, w, b, v, u_
             nc.vector.tensor_copy(out=ident_h[:], in_=ident[:])
             nc.gpsimd.memset(u_s[:].rearrange("p g n -> p (g n)").bitcast(I32), 0)
 
-            nc.scalar.dma_start(out=x_sc[:], in_=x_scale.rearrange("(r p) d -> p r d", p=P))
+            x_sc_rows = x_scale.rearrange("(r p) d -> p r d", p=P)
+            nc.scalar.dma_start(out=x_sc[:, 0:4, :], in_=x_sc_rows[:, 0:4, :])
             xb = []
             for r in range(8):
                 xb.append(work.tile([P, K], U8, name="xb", bufs=8))
@@ -76,6 +77,7 @@ def tile_biaffine_contact_transposed_d4_kernel(tc, x_bytes, x_scale, w, b, v, u_
                 load_x(r)
             for g in range(PASSES):
                 load_w(g)
+            nc.sync.dma_start(out=x_sc[:, 4:8, :], in_=x_sc_rows[:, 4:8, :])
             for r in range(4, 8):
                 load_x(r)
             nc.sync.dma_start(out=b_raw[:], in_=b.rearrange("(g p t) -> p g t", p=P, t=4))
@@ -194,11 +196,12 @@ def tile_biaffine_contact_transposed_d4_kernel(tc, x_bytes, x_scale, w, b, v, u_
                 split = ("E", ch, G, 0) in on_s
                 if (ch, G) not in hs:
                     name = "hs%d" % G if ch == 0 else "wr%d" % (2 + ch)
-                    if ch == 0 or G == 0:
+                    if ch == 0:
                         hs[ch, G] = work.tile([P, 4, HALF], F32 if split else BF16, name=name, bufs=1)
-                    else:
-                        hs[ch, G] = hs[ch, 0]
-                dst = hs[ch, G][:, t, 256 * G * (ch > 0) : 256 * G * (ch > 0) + wide[ch]]
+                    elif G == 0:
+                        both = work.tile([P, 2, 4, 256], F32 if split else BF16, name=name, bufs=1)
+                        hs[ch, 0], hs[ch, 1] = both[:, 0, :, :], both[:, 1, :, :]
+                dst = hs[ch, G][:, t, :]
                 if split:
                     nc.scalar.activation(out=dst, in_=bank_of["Y", ch, G, t], func=IDENT, bias=b_raw[:, G, t : t + 1], scale=1.0)
                 else:
@@ -214,7 +217,7 @@ def tile_biaffine_contact_transposed_d4_kernel(tc, x_bytes, x_scale, w, b, v, u_
             def h_mix(eng, ch, G, k):
                 if (ch, G) not in hg:
                     hg[ch, G] = work.tile([P, wide[ch], 4], BF16, name="hg%d" % G, bufs=1, align_bytes=64)
-                c0 = 256 * G * (ch > 0) + 256 * k
+                c0 = 256 * k
                 i0 = span[ch].start + 256 * k
                 dst = hg[ch, G][:, 256 * k : 256 * k + 256, :]
                 src = hs[ch, G][:, :, c0 : c0 + 256]
@@ -267,7 +270,7 @@ def tile_biaffine_contact_transposed_d4_kernel(tc, x_bytes, x_scale, w, b, v, u_
                 nc.sync.dma_start(out=out[P * jt : P * jt + P, HALF * h : HALF * h + HALF], in_=o_tile[zq.index((h, jt)) // 4][:, zq.index((h, jt)) % 4, :])
 
             vec, sca, pe, place = [], [], [], {}
-            on_s = {("A", 0, 4), ("A", 1, 4)}
+            on_s = {("A", 0, 4), ("A", 1, 4), ("A", 2, 4)}
             on_s |= {("E", ch, G, 0) for ch in range(3) for G in range(2)}
             passes = {(ch, G): (0, 1, 2, 3, 4) for ch in range(3) for G in range(2)}
             passes[0, 1] = (0, 3, 1, 4, 2)
@@ -295,8 +298,7 @@ def tile_biaffine_contact_transposed_d4_kernel(tc, x_bytes, x_scale, w, b, v, u_
             a(sca, ("C", 1, 0), ("C", 0, 1), ("C", 3, 0))
             a(vec, ("W", 0, 1), ("C", 4, 0), ("W", 3, 0), ("W", 4, 0))
             a(sca, ("C", 1, 1), ("C", 2, 1))
-            a(vec, ("C", 3, 1), ("C", 4, 1), ("W", 3, 1), ("W", 1, 1), ("W", 4, 1))
-            a(vec, ("W", 2, 1))
+            a(vec, ("C", 3, 1), ("C", 4, 1), ("W", 3, 1), ("W", 1, 1), ("W", 4, 1), ("W", 2, 1))
             for G in range(2):
                 for i, g in enumerate(passes[0, G]):
                     for t in range(4):
@@ -319,45 +321,65 @@ def tile_biaffine_contact_transposed_d4_kernel(tc, x_bytes, x_scale, w, b, v, u_
                 a(sca, ("E", 0, 0, t))
             for i in range(10):
                 place["T", 2 + i // 5, i % 5] = (0, 1, 2, 3, 0, 1, 0, 1, 0, 1)[i]
+            a(sca, ("A", 2, 4))
             for g in range(5):
-                a(vec, ("A", 2, g))
+                if g < 4:
+                    a(vec, *[("A", 2, g)][g < 0 :])
                 a(pe, ("T", 2, g))
-                if g == 1:
+                if g == 2:
                     a(pe, *last)
                 a(sca, ("B", 2, g))
             a(sca, ("k",))
             for t in range(4):
                 a(sca, ("E", 0, 1, t))
-            a(vec, ("X", 1, 0), ("X", 1, 1), ("A", 3, 0), ("X", 1, 2), ("X", 1, 3), ("A", 3, 1), ("X", 1, 4))
-            a(vec, ("A", 3, 2), ("A", 3, 3), ("A", 3, 4), ("M", 0, 0, 0), ("X", 2, 0), ("X", 2, 1), ("M", 0, 0, 1), ("X", 2, 2), ("X", 2, 3), ("X", 2, 4), ("H", 0, 0), ("M", 0, 1, 0), ("M", 0, 1, 1), ("H", 0, 1))
-
+            a(vec, ("M", 0, 0, 0), ("X", 1, 0), ("X", 1, 1), ("X", 1, 2), ("X", 1, 3), ("X", 1, 4), ("M", 0, 0, 1), ("H", 0, 0), ("M", 0, 1, 0), ("M", 0, 1, 1), ("H", 0, 1))
             a(pe, ("K",))
 
-            def y256(ch, G, homes, turns=()):
-                turns = list(turns)
+            def y256(ch, G, homes):
                 for t0 in (0, 2):
                     for g in passes[ch, G]:
                         for t in (t0, t0 + 1):
                             a(pe, ("Y", ch, G, t, g))
-                    for n in turns[t0 : t0 + 2] if t0 == 0 else turns[2:]:
-                        a(pe, ("T", 3, n))
-                        a(sca, ("B", 3, n))
                     for t in (t0, t0 + 1):
                         a(sca, ("E", ch, G, t))
                 for t in range(4):
                     place["Y", ch, G, t] = (homes[t % 2], 256 * (t // 2))
 
-            y256(1, 0, (2, 3), (0, 1, 2, 3, 4))
+            y256(1, 0, (2, 3))
             y256(1, 1, (4, 5))
-            y256(2, 0, (2, 3))
-            y256(2, 1, (4, 5))
-            nz = z(4, (6, 7, 0, 1))
-            for ch in (1, 2):
-                for G in range(2):
-                    a(vec, ("M", ch, G, 0), ("H", ch, G))
-            nz = z(28, (6, 7, 0, 1, 2, 3, 4, 5))
-            f(0, 13, "S")
-            f(13, 32, "SV")
+            ring = (6, 7, 0, 1)
+            fd = 0
+            for i in range(4):
+                place[("O",) + zq[i]] = ring[i]
+            for G in range(2):
+                for i in range(4):
+                    a(pe, ("Z",) + zq[i] + (G,))
+            nz = 4
+            f(0, 3, "S")
+            fd = 3
+            for g in range(5):
+                a(vec, ("A", 3, g))
+                if g >= 2:
+                    a(vec, ("X", 2, g - 2))
+                nz = z(1, ring)
+                a(pe, ("T", 3, g))
+                place["T", 3, g] = (2, 3, 4, 5, 2)[g]
+                if g:
+                    a(sca, ("B", 3, g - 1))
+                f(fd, nz - 1, "S")
+                fd = nz - 1
+            a(sca, ("B", 3, 4))
+            a(vec, ("X", 2, 3), ("M", 1, 0, 0), ("X", 2, 4), ("H", 1, 0), ("M", 1, 1, 0), ("H", 1, 1))
+            nz = z(2, ring)
+            f(fd, nz, "S")
+            fd = nz
+            y256(2, 0, (3, 4))
+            y256(2, 1, (5, 2))
+            a(vec, ("M", 2, 0, 0), ("H", 2, 0), ("M", 2, 1, 0), ("H", 2, 1))
+            nz = z(16 - nz, ring)
+            f(fd, 16, "S")
+            nz = z(16, (3, 4, 5, 2, 6, 7, 0, 1))
+            f(16, 32, "SV")
             make = {
                 "A": widen, "T": turn, "B": x_out, "X": x_quant, "C": w_mix, "W": w_quant, "K": spread, "k": spread_out,
                 "Y": mul1, "E": h_bias, "M": h_mix, "H": h_quant, "Z": mul2, "F": finish, "D": store,

from contextlib import ExitStack

import concourse.mybir as mybir
from concourse.masks import make_identity

L, K, F, J = 1024, 2560, 1024, 2048
FLOPS = 2 * L * K * F + 2 * J * F * L

F32 = mybir.dt.float32
BF16 = mybir.dt.bfloat16
U8 = mybir.dt.uint8
U32 = mybir.dt.uint32
I32 = mybir.dt.int32
E4M3 = mybir.dt.float8_e4m3fn
E4M3X4 = mybir.dt.float8_e4m3fn_x4
E2M1X4 = mybir.dt.float4_e2m1fn_x4
MULT = mybir.AluOpType.mult
ADD = mybir.AluOpType.add
COPY = mybir.ActivationFunctionType.Copy
IDENT = mybir.ActivationFunctionType.Identity

P = 128
PASSES = K // 512
HALF = 512
GROUPS = F // 512
WG = {"V": 2, "S": 3}


def tile_biaffine_contact_transposed_d4_kernel(tc, x_bytes, x_scale, w, b, v, u_words, u_scales, c, out):
    nc = tc.nc
    with ExitStack() as ctx:
        keep = ctx.enter_context(tc.tile_pool(name="keep", bufs=1))
        work = ctx.enter_context(tc.tile_pool(name="work", bufs=2))
        psum = ctx.enter_context(tc.psum_pool(name="psum", bufs=1))

        def bank(i):
            return psum.tile([P, 512], F32, name="bank%d" % i)

        x_sc = keep.tile([P, 8, 20], F32, name="x_sc")
        ident = keep.tile([P, P], F32, name="ident")
        v_all = keep.tile([P, L], BF16, name="v_all")
        b_raw = keep.tile([P, GROUPS, 4], BF16, name="b_raw")
        c_row = keep.tile([P, P], BF16, name="c_row")
        ident_h = keep.tile([P, P], BF16, name="ident_h")
        c_col = keep.tile([P, 16], F32, name="c_col")
        x_codes = keep.tile([P, PASSES, L], U32, name="x_codes", align_bytes=64)
        x_planes = keep.tile([P, PASSES, L], U8, name="x_planes", align_bytes=64)
        w_codes = keep.tile([P, PASSES, F], U32, name="w_codes", align_bytes=64)
        w_planes = keep.tile([P, PASSES, F], U8, name="w_planes", align_bytes=64)
        h_codes = keep.tile([P, GROUPS, L], U32, name="h_codes", align_bytes=64)
        h_planes = keep.tile([P, GROUPS, L], U8, name="h_planes", align_bytes=64)
        u_w = keep.tile([P, GROUPS, 2 * J], U8, name="u_w", align_bytes=64)
        u_s = keep.tile([P, GROUPS, J], U8, name="u_s", align_bytes=64)

        with tc.manual_schedule():
            make_identity(nc, ident[:])
            nc.vector.memset(c_row[:], 0.0)
            nc.vector.tensor_copy(out=ident_h[:], in_=ident[:])
            nc.gpsimd.memset(u_s[:].rearrange("p g n -> p (g n)").bitcast(I32), 0)

            x_sc_rows = x_scale.rearrange("(r p) d -> p r d", p=P)
            nc.scalar.dma_start(out=x_sc[:, 0:4, :], in_=x_sc_rows[:, 0:4, :])
            xb = []
            for r in range(8):
                xb.append(work.tile([P, K], U8, name="xb", bufs=8))
            wr = []

            def load_x(r):
                nc.sync.dma_start(out=xb[r][:], in_=x_bytes[P * r : P * r + P, :])

            def load_w(g):
                t = work.tile([P, 4, F], BF16, name="wr%d" % g, bufs=1)
                nc.sync.dma_start(out=t[:], in_=w[512 * g : 512 * g + 512, :].rearrange("(p j) f -> p j f", j=4))
                wr.append(t)

            for r in range(4):
                load_x(r)
            for g in range(PASSES):
                load_w(g)
            nc.sync.dma_start(out=x_sc[:, 4:8, :], in_=x_sc_rows[:, 4:8, :])
            for r in range(4, 8):
                load_x(r)
            nc.sync.dma_start(out=b_raw[:], in_=b.rearrange("(g p t) -> p g t", p=P, t=4))
            nc.sync.dma_start(out=c_row[0:16, :], in_=c.rearrange("(j p) -> j p", p=P))
            for g in range(GROUPS):
                nc.sync.dma_start(out=u_w[:, g, :].bitcast(I32), in_=u_words[g].bitcast(I32))
            for q in range(4):
                nc.sync.dma_start(
                    out=u_s[32 * q : 32 * q + 4, :, :].bitcast(I32),
                    in_=u_scales[:, 4 * q : 4 * q + 4, :].rearrange("g q n -> q g n").bitcast(I32),
                )
            nc.sync.dma_start(out=v_all[:], in_=v.partition_broadcast(128))

            xw, xg, wg, hs, hg, o_tile = {}, {}, {}, {}, {}, {}
            bank_of, bank_now = {}, {}
            wide = (512, 256, 256)
            span = (slice(0, 512), slice(512, 768), slice(768, 1024))
            wg_count = {"V": 0, "S": 0}

            def widen(eng, pair, g):
                for r in (2 * pair, 2 * pair + 1):
                    if r not in xw:
                        xw[r] = work.tile([P, PASSES, 2, P, 2], BF16, name="xw%d" % (r % 4), bufs=1, align_bytes=64)
                    for q in range(4):
                        d = 4 * g + q
                        byte = xb[r][:, 128 * d : 128 * d + 128].bitcast(E4M3)
                        if eng == "S":
                            nc.scalar.activation(
                                out=xw[r][:, g, :, :, :].rearrange("p u m e -> p (u m e)")[:, 128 * q : 128 * q + 128],
                                in_=byte,
                                func=COPY,
                                scale=x_sc[:, r, d : d + 1],
                            )
                        else:
                            nc.vector.tensor_scalar(
                                out=xw[r][:, g, :, 32 * q : 32 * q + 32, :].rearrange("p u m e -> p m u e"),
                                in0=byte.rearrange("p (m u e) -> p m u e", u=2, e=2),
                                scalar1=x_sc[:, r, d : d + 1],
                                scalar2=None,
                                op0=MULT,
                            )

            def turn(eng, pair, g):
                bank_of["T", pair, g] = bank(place["T", pair, g])
                tv = bank_of["T", pair, g][:].rearrange("p (u r) -> p u r", u=2)
                for k, r in enumerate((2 * pair, 2 * pair + 1)):
                    for u in range(2):
                        if ("A", pair, g) in on_s:
                            words = xw[r][:, g, :, :, :].rearrange("p u m e -> p (u m e)").bitcast(F32)[:, u::2]
                        else:
                            words = xw[r][:, g, u, :, :].rearrange("p m e -> p (m e)").bitcast(F32)
                        nc.tensor.transpose(tv[:, u, P * k : P * k + P], words, ident[:])

            def x_out(eng, pair, g):
                ch = max(0, pair - 1)
                k, n = (pair, 2) if ch == 0 else (0, 1)
                if (ch, g) not in xg:
                    xg[ch, g] = work.tile([P, 256 * n, 4], BF16, name="xg%d" % g, bufs=1, align_bytes=64)
                dst = xg[ch, g][:, 256 * k : 256 * k + 256, :].rearrange("p r j -> p (r j)").bitcast(F32).rearrange("p (r u) -> p r u", u=2)
                src = bank_of["T", pair, g][:].rearrange("p (u r) -> p r u", u=2)
                if eng == "S":
                    nc.scalar.copy(out=dst, in_=src)
                else:
                    nc.vector.tensor_copy(out=dst, in_=src)

            def x_quant(eng, ch, g):
                nc.vector.quantize_mx(
                    out=x_codes[:, g, span[ch]].bitcast(E4M3X4),
                    scales=x_planes[:, g, span[ch]],
                    in_=xg[ch, g][:].rearrange("p r j -> p (r j)"),
                )

            def w_mix(eng, g, G):
                t = work.tile([P, 4, P, 4], BF16, name="wg%s%d" % (eng, wg_count[eng] % WG[eng]), bufs=1, align_bytes=64)
                wg_count[eng] += 1
                wg[g, G] = t
                dst = t[:].rearrange("p t m j -> p m j t")
                src = wr[g][:, :, 512 * G : 512 * G + 512].rearrange("p j (m t) -> p m j t", t=4)
                if eng == "S":
                    nc.scalar.copy(out=dst, in_=src)
                else:
                    nc.vector.tensor_copy(out=dst, in_=src)

            def w_quant(eng, g, G):
                nc.vector.quantize_mx(
                    out=w_codes[:, g, 512 * G : 512 * G + 512].bitcast(E4M3X4),
                    scales=w_planes[:, g, 512 * G : 512 * G + 512],
                    in_=wg[g, G][:].rearrange("p t m j -> p (t m j)"),
                )

            def spread(eng):
                bank_of["c"] = psum.tile([P, 2 * HALF], BF16, name="bank1")
                nc.tensor.transpose(bank_of["c"][:, 0:P], c_row[:], ident_h[:])

            def spread_out(eng):
                nc.scalar.copy(out=c_col[:], in_=bank_of["c"][:, 0:16])

            def mul1(eng, ch, G, t, g):
                home, col = place["Y", ch, G, t]
                if g == passes[ch, G][0]:
                    if col == 0:
                        bank_now[home] = bank(home)
                    bank_of["Y", ch, G, t] = bank_now[home][:, col : col + wide[ch]]
                f = 512 * G + P * t
                nc.tensor.matmul_mx(
                    out=bank_of["Y", ch, G, t],
                    lhsT=w_codes[:, g, f : f + P].bitcast(E4M3X4),
                    lhsT_scale=w_planes[:, g, f : f + P],
                    rhs=x_codes[:, g, span[ch]].bitcast(E4M3X4),
                    rhs_scale=x_planes[:, g, span[ch]],
                    start=(g == passes[ch, G][0]),
                    stop=(g == passes[ch, G][-1]),
                )

            def h_bias(eng, ch, G, t):
                split = ("E", ch, G, 0) in on_s
                if (ch, G) not in hs:
                    name = "hs%d" % G if ch == 0 else "wr%d" % (2 + ch)
                    if ch == 0:
                        hs[ch, G] = work.tile([P, 4, HALF], F32 if split else BF16, name=name, bufs=1)
                    elif G == 0:
                        both = work.tile([P, 2, 4, 256], F32 if split else BF16, name=name, bufs=1)
                        hs[ch, 0], hs[ch, 1] = both[:, 0, :, :], both[:, 1, :, :]
                dst = hs[ch, G][:, t, :]
                if split:
                    nc.scalar.activation(out=dst, in_=bank_of["Y", ch, G, t], func=IDENT, bias=b_raw[:, G, t : t + 1], scale=1.0)
                else:
                    nc.vector.scalar_tensor_tensor(
                        out=dst,
                        in0=bank_of["Y", ch, G, t],
                        scalar=b_raw[:, G, t : t + 1],
                        in1=v_all[:, span[ch]],
                        op0=ADD,
                        op1=MULT,
                    )

            def h_mix(eng, ch, G, k):
                if (ch, G) not in hg:
                    hg[ch, G] = work.tile([P, wide[ch], 4], BF16, name="hg%d" % G, bufs=1, align_bytes=64)
                c0 = 256 * k
                i0 = span[ch].start + 256 * k
                dst = hg[ch, G][:, 256 * k : 256 * k + 256, :]
                src = hs[ch, G][:, :, c0 : c0 + 256]
                if ("E", ch, G, 0) in on_s:
                    nc.vector.tensor_tensor(
                        out=dst,
                        in0=src.rearrange("p t i -> p i t"),
                        in1=v_all[:, i0 : i0 + 256].unsqueeze(2).to_broadcast([P, 256, 4]),
                        op=MULT,
                    )
                else:
                    dst = dst.rearrange("p (c i) t -> p c t i", i=4)
                    src = src.rearrange("p t (c i) -> p c t i", i=4)
                    if eng == "S":
                        nc.scalar.copy(out=dst, in_=src)
                    else:
                        nc.vector.tensor_copy(out=dst, in_=src)

            def h_quant(eng, ch, G):
                nc.vector.quantize_mx(
                    out=h_codes[:, G, span[ch]].bitcast(E4M3X4),
                    scales=h_planes[:, G, span[ch]],
                    in_=hg[ch, G][:].rearrange("p i t -> p (i t)"),
                )

            def mul2(eng, h, jt, G):
                if G == 0:
                    bank_of["O", h, jt] = bank(place["O", h, jt])
                nc.tensor.matmul_mx(
                    out=bank_of["O", h, jt][:],
                    lhsT=u_w[:, G, 256 * jt : 256 * jt + 256].bitcast(E2M1X4),
                    lhsT_scale=u_s[:, G, P * jt : P * jt + P],
                    rhs=h_codes[:, G, HALF * h : HALF * h + HALF].bitcast(E4M3X4),
                    rhs_scale=h_planes[:, G, HALF * h : HALF * h + HALF],
                    start=(G == 0),
                    stop=(G == GROUPS - 1),
                )

            def finish(eng, h, jt):
                i = zq.index((h, jt))
                if i // 4 not in o_tile:
                    o_tile[i // 4] = work.tile([P, 4, HALF], F32, name="wr%d" % (i // 4 % 3), bufs=1)
                t = o_tile[i // 4][:, i % 4, :]
                if eng == "S":
                    nc.scalar.activation(out=t, in_=bank_of["O", h, jt][:], func=IDENT, bias=c_col[:, jt : jt + 1], scale=1.0)
                else:
                    nc.vector.tensor_scalar(out=t, in0=bank_of["O", h, jt][:], scalar1=c_col[:, jt : jt + 1], scalar2=None, op0=ADD)

            def store(eng, h, jt):
                nc.sync.dma_start(out=out[P * jt : P * jt + P, HALF * h : HALF * h + HALF], in_=o_tile[zq.index((h, jt)) // 4][:, zq.index((h, jt)) % 4, :])

            vec, sca, pe, place = [], [], [], {}
            on_s = {("A", 0, 4), ("A", 1, 4), ("A", 2, 4)}
            on_s |= {("E", ch, G, 0) for ch in range(3) for G in range(2)}
            passes = {(ch, G): (0, 1, 2, 3, 4) for ch in range(3) for G in range(2)}
            passes[0, 1] = (0, 3, 1, 4, 2)

            def a(q, *ss):
                q.extend(ss)

            a(sca, ("A", 0, 4))
            for g in range(4):
                a(vec, ("A", 0, g))
            for g in range(4):
                a(vec, ("A", 1, g))
            for g in range(5):
                a(pe, ("T", 0, g))
            for g in range(5):
                a(pe, ("T", 1, g))
            for i in range(10):
                place["T", i // 5, i % 5] = i % 5
            a(sca, ("B", 0, 0), ("B", 0, 1), ("A", 1, 4))
            a(sca, ("B", 0, 2), ("B", 0, 3), ("B", 0, 4))
            for g in range(5):
                a(sca, ("B", 1, g))
            last = []
            a(vec, ("C", 0, 0), ("X", 0, 0), ("X", 0, 1), ("W", 0, 0), ("X", 0, 2), ("C", 2, 0), ("W", 1, 0), ("X", 0, 3), ("X", 0, 4), ("W", 2, 0))
            a(sca, ("C", 1, 0), ("C", 0, 1), ("C", 3, 0))
            a(vec, ("W", 0, 1), ("C", 4, 0), ("W", 3, 0), ("W", 4, 0))
            a(sca, ("C", 1, 1), ("C", 2, 1))
            a(vec, ("C", 3, 1), ("C", 4, 1), ("W", 3, 1), ("W", 1, 1), ("W", 4, 1), ("W", 2, 1))
            for G in range(2):
                for i, g in enumerate(passes[0, G]):
                    for t in range(4):
                        a(last if (G, i) == (1, 4) else pe, ("Y", 0, G, t, g))
                        place["Y", 0, G, t] = (4 * G + t, 0)
            zq = [(h, jt) for h in range(2) for jt in range(16)]
            nz = 0

            def z(n, homes):
                for i in range(nz, nz + n):
                    place[("O",) + zq[i]] = homes[i % len(homes)]
                    a(pe, ("Z",) + zq[i] + (0,), ("Z",) + zq[i] + (1,))
                return nz + n

            def f(lo, hi, eng):
                for i in range(lo, hi):
                    a(vec if eng[i % len(eng)] == "V" else sca, ("F",) + zq[i])

            for t in range(4):
                a(sca, ("E", 0, 0, t))
            for i in range(10):
                place["T", 2 + i // 5, i % 5] = (0, 1, 2, 3, 0, 1, 0, 1, 0, 1)[i]
            a(sca, ("A", 2, 4))
            for g in range(5):
                if g < 4:
                    a(vec, *[("A", 2, g)][g < 0 :])
                a(pe, ("T", 2, g))
                if g == 2:
                    a(pe, *last)
                a(sca, ("B", 2, g))
            a(sca, ("k",))
            for t in range(4):
                a(sca, ("E", 0, 1, t))
            a(vec, ("M", 0, 0, 0), ("X", 1, 0), ("X", 1, 1), ("X", 1, 2), ("X", 1, 3), ("X", 1, 4), ("M", 0, 0, 1), ("H", 0, 0), ("M", 0, 1, 0), ("M", 0, 1, 1), ("H", 0, 1))
            a(pe, ("K",))

            def y256(ch, G, homes):
                for t0 in (0, 2):
                    for g in passes[ch, G]:
                        for t in (t0, t0 + 1):
                            a(pe, ("Y", ch, G, t, g))
                    for t in (t0, t0 + 1):
                        a(sca, ("E", ch, G, t))
                for t in range(4):
                    place["Y", ch, G, t] = (homes[t % 2], 256 * (t // 2))

            y256(1, 0, (2, 3))
            y256(1, 1, (4, 5))
            ring = (6, 7, 0, 1)
            fd = 0
            for i in range(4):
                place[("O",) + zq[i]] = ring[i]
            for G in range(2):
                for i in range(4):
                    a(pe, ("Z",) + zq[i] + (G,))
            nz = 4
            f(0, 3, "S")
            fd = 3
            for g in range(5):
                a(vec, ("A", 3, g))
                if g >= 2:
                    a(vec, ("X", 2, g - 2))
                nz = z(1, ring)
                a(pe, ("T", 3, g))
                place["T", 3, g] = (2, 3, 4, 5, 2)[g]
                if g:
                    a(sca, ("B", 3, g - 1))
                f(fd, nz - 1, "S")
                fd = nz - 1
            a(sca, ("B", 3, 4))
            a(vec, ("X", 2, 3), ("M", 1, 0, 0), ("X", 2, 4), ("H", 1, 0), ("M", 1, 1, 0), ("H", 1, 1))
            nz = z(2, ring)
            f(fd, nz, "S")
            fd = nz
            y256(2, 0, (3, 4))
            y256(2, 1, (5, 2))
            a(vec, ("M", 2, 0, 0), ("H", 2, 0), ("M", 2, 1, 0), ("H", 2, 1))
            nz = z(16 - nz, ring)
            f(fd, 16, "S")
            nz = z(16, (3, 4, 5, 2, 6, 7, 0, 1))
            f(16, 32, "SV")
            make = {
                "A": widen, "T": turn, "B": x_out, "X": x_quant, "C": w_mix, "W": w_quant, "K": spread, "k": spread_out,
                "Y": mul1, "E": h_bias, "M": h_mix, "H": h_quant, "Z": mul2, "F": finish, "D": store,
            }
            reader = {}
            for s in pe:
                if s[0] == "T":
                    reader[s] = [("B",) + s[1:]]
                elif s[0] == "K":
                    reader[s] = [("k",)]
                elif s[0] == "Y" and s[4] == passes[s[1:3]][0]:
                    reader[s] = [("E",) + s[1:4]]
                elif s[0] == "Z" and s[3] == 0:
                    reader[s] = [("F",) + s[1:3]]
            needs = {}
            last = {}
            for s in pe:
                n = []
                if s in reader:
                    if s[0] == "T":
                        homes = [place[s]]
                    elif s[0] == "K":
                        homes = [1]
                    elif s[0] == "Y":
                        homes = [place[s[0:4]][0]]
                    else:
                        homes = [place[("O",) + s[1:3]]]
                    for home in homes:
                        if s[0] == "Y" and place[s[0:4]][1]:
                            last[home] = last[home] + reader[s]
                        else:
                            n += last.get(home, [])
                            last[home] = reader[s]
                if s[0] == "T":
                    n.append(("A",) + s[1:])
                elif s[0] == "Y":
                    n += [("W", s[4], s[2]), ("X", s[1], s[4])]
                elif s[0] == "Z":
                    n += [("H", ch, s[3]) for ch in ((0,) if s[1] == 0 else (1, 2))]
                needs[s] = n
            for q in (vec, sca):
                mixes = [s for s in q if s[0] == "C"]
                for s in q:
                    n = []
                    if s[0] == "A" and s[1] >= 2:
                        n = [("T", s[1] - 2, g) for g in range(PASSES)]
                    elif s[0] == "B":
                        n = [("T",) + s[1:]] + ([("X", s[1] - 2, s[2])] if s[1] >= 2 else [])
                    elif s[0] == "X":
                        n = [("B", s[1] + 1, s[2])] + ([("B", 0, s[2])] if s[1] == 0 else [])
                    elif s[0] == "C":
                        i, ring = mixes.index(s), WG["V" if q is vec else "S"]
                        n = [("W",) + mixes[i - ring][1:]] if i >= ring else []
                    elif s[0] == "W":
                        n = [("C",) + s[1:]]
                    elif s[0] == "k":
                        n = [("K",)]
                    elif s[0] == "E":
                        n = [("Y",) + s[1:4] + (passes[s[1:3]][-1],)]
                        if s[1] > 0:
                            n += [("W", 2 + s[1], 0), ("W", 2 + s[1], 1)]
                    elif s[0] == "M":
                        n = [("E", s[1], s[2], t) for t in range(4)]
                        if s[1] > 0:
                            n.append(("H", s[1] - 1, s[2]))
                    elif s[0] == "H":
                        n = [("M",) + s[1:3] + (k,) for k in range(2 if s[1] == 0 else 1)]
                    elif s[0] == "F":
                        n = [("Z",) + s[1:3] + (1,), ("k",)]
                        i = zq.index(s[1:]) // 4 - 3
                        n += [("D",) + z for z in zq[4 * i : 4 * i + 4]] if i >= 0 else [("W", i + 3, 0), ("W", i + 3, 1)]
                    needs[s] = n
            sto = [("D",) + z for z in zq]
            for s in sto:
                needs[s] = [("F",) + s[1:]]
            said = set()
            queues = [["V", vec, 0], ["S", sca, 0], ["T", pe, 0], ["D", sto, 0]]
            left = len(vec) + len(sca) + len(pe) + len(sto)
            assert len(needs) == left, (len(needs), left)
            while left:
                before = left
                for q in queues:
                    while q[2] < len(q[1]) and all(n in said for n in needs[q[1][q[2]]]):
                        s = q[1][q[2]]
                        make[s[0]](q[0], *s[1:])
                        said.add(s)
                        q[2] += 1
                        left -= 1
                assert left < before, [q[1][q[2]] for q in queues if q[2] < len(q[1])]
